import numpy as np
import ml_dtypes


def mxq(x, axis, fmt="e4m3"):
    dtype, down = {"e4m3": (ml_dtypes.float8_e4m3fn, 7), "e5m2": (ml_dtypes.float8_e5m2, 14)}[fmt]
    v = np.moveaxis(np.asarray(x, np.float32).astype(ml_dtypes.bfloat16).astype(np.float64), axis, -1)
    blocks = v.reshape(v.shape[:-1] + (-1, 32))
    amax = np.abs(blocks).max(-1, keepdims=True)
    byte = np.maximum(np.where(amax > 0, np.frexp(amax)[1] - 1 + 127, 0) - down, 1)
    scale = np.exp2(byte - 127.0)
    codes = (blocks / scale).astype(np.float32).astype(dtype).astype(np.float64)
    return np.moveaxis((codes * scale).reshape(v.shape), -1, axis)


WIDE = False


def mx_kscale(k):
    if not WIDE:
        return np.ones(k)
    levels = np.array([10, -10, 5, -5, 0])
    if k % 512:
        return np.exp2(np.random.permutation(np.resize(levels, k // 32))).repeat(32)
    a = np.empty((k // 512, 16))
    for p in range(k // 512):
        a[p, :8] = np.random.permutation(np.resize(levels, 8))
        for g in range(8):
            far = levels[np.abs(levels - a[p, g]) >= 10]
            a[p, g + 8] = far[np.random.randint(len(far))]
    return np.exp2(a.ravel()).repeat(32)


def f64(x):
    return np.asarray(x).astype(np.float64)


def striped(idx):
    return np.tile(idx.reshape(-1, 16).T, (8, 1)).astype(np.uint16)


def unstriped(offs):
    return offs[:16].T.reshape(-1).astype(np.int64)


def pack_weight(w):
    k, n = w.shape
    w = f64(np.asarray(w, np.float32).astype(ml_dtypes.bfloat16)).reshape(k // 32, 32, n)
    amax = np.abs(w).max(1)
    byte = np.clip(np.where(amax > 0, np.frexp(amax)[1] - 1 + 127 - 7, 1), 1, 254)
    scaled = (w * np.exp2(127.0 - byte)[:, None, :]).reshape(k, n).astype(np.float32)
    words = np.ascontiguousarray(scaled.reshape(k // 512, 128, 4, n).transpose(0, 1, 3, 2)).astype(ml_dtypes.float8_e4m3fn).view(np.uint8)
    return words, np.ascontiguousarray(byte.astype(np.uint8).reshape(k // 512, 16, n))


def unpack_weight(words, scales):
    g, p, n, _ = words.shape
    vals = np.ascontiguousarray(words).view(ml_dtypes.float8_e4m3fn).astype(np.float64) * np.repeat(np.exp2(scales.astype(np.float64) - 127.0), 8, axis=1)[..., None]
    return vals.transpose(0, 1, 3, 2).reshape(g * 512, n)


K, T, S, N, V, W, U = 1024, 1024, 512, 256, 256, 768, 512


def setup_inputs():
    n = np.random.standard_normal
    s = mx_kscale(K)[:, None]
    packed_xT = pack_weight(n((K, T)) * s)
    return {
        "x_words": packed_xT[0],
        "x_scales": packed_xT[1],
        "w1": (n((K, N)) / np.sqrt(K) / s).astype(np.float32),
        "offs": striped(np.random.permutation(T)[:S]),
        "ea": striped(np.random.randint(0, S, V)),
        "eb": striped(np.random.randint(0, S, V)),
        "wa": striped(np.random.randint(0, S, V)),
        "wb": striped(np.random.randint(0, S, V)),
        "fa": striped(np.random.randint(0, W, U)),
        "fb": striped(np.random.randint(0, W, U)),
    }


def reference(x_words, x_scales, w1, offs, ea, eb, wa, wb, fa, fb):
    xq = unpack_weight(x_words, x_scales)[:, unstriped(offs)]
    y = mxq(f64(w1), 0, "e4m3").T @ xq
    edge = 0.375 * (y[:, unstriped(ea)] + y[:, unstriped(eb)]) + 0.125 * (y[:, unstriped(wa)] + y[:, unstriped(wb)])
    fine = np.concatenate([y, edge], axis=1)
    return 0.5 * (fine[:, unstriped(fa)] + fine[:, unstriped(fb)]) + 0.25 * (np.abs(fine[:, unstriped(fa)] - fine[:, unstriped(fb)]))

@@ -1,0 +1,157 @@
+from contextlib import ExitStack
+
+import concourse.mybir as mybir
+
+K, T, S, N, V, W, U = 1024, 1024, 512, 256, 256, 768, 512
+FLOPS = 2 * K * S * N
+
+F32 = mybir.dt.float32
+BF16 = mybir.dt.bfloat16
+I32 = mybir.dt.int32
+U32 = mybir.dt.uint32
+U16 = mybir.dt.uint16
+U8 = mybir.dt.uint8
+FP8X4 = mybir.dt.float8_e4m3fn_x4
+ALU = mybir.AluOpType
+COPY = mybir.ActivationFunctionType.Copy
+
+P = 128
+PACK = 4
+PASSES = K // (P * PACK)
+BLOCKS = N // P
+PIECES = ((0, 256), (256, 384), (384, 512))
+HALF = U // 2
+
+
+def entries(list_tile, lo, hi):
+    return list_tile[:, lo // 16 : hi // 16]
+
+
+def tile_picked_yloopsd_fine_p_kernel(tc, x_words, x_scales, w1, offs, ea, eb, wa, wb, fa, fb, out):
+    nc = tc.nc
+    with ExitStack() as ctx:
+        keep = ctx.enter_context(tc.tile_pool(name="keep", bufs=1))
+        psum = ctx.enter_context(tc.psum_pool(name="psum", bufs=1))
+
+        def load_list(name, src):
+            tile = keep.tile([P, src.shape[1]], U16, name=name)
+            nc.sync.dma_start(tile[:], src)
+            return tile
+
+        scale_table = keep.tile([P, T], U8, align_bytes=64)
+        nc.vector.memset(scale_table[:].bitcast(I32), 0)
+        offs_sb = load_list("offs_sb", offs)
+        for q in range(4):
+            nc.sync.dma_start(
+                scale_table[32 * q : 32 * q + 4 * PASSES, :].bitcast(I32),
+                x_scales[:, 4 * q : 4 * q + 4, :].bitcast(I32),
+            )
+
+        word_table = [keep.tile([P, T], I32, name=f"word_table{a}", align_bytes=64) for a in range(PASSES)]
+        w_raw = [keep.tile([P, PACK, N], F32, name=f"w_raw{a}", align_bytes=64) for a in range(PASSES)]
+
+        def load_words(a):
+            nc.sync.dma_start(word_table[a][:], x_words[a].rearrange("p n t -> p (n t)").bitcast(I32))
+
+        load_words(0)
+        for a in range(PASSES):
+            nc.sync.dma_start(w_raw[a][:], w1[a * 512 : (a + 1) * 512, :].rearrange("(p j) m -> p j m", j=PACK))
+        load_words(1)
+        ea_sb, eb_sb, wa_sb, wb_sb, fa_sb, fb_sb = (
+            load_list(name, src)
+            for name, src in (("ea_sb", ea), ("eb_sb", eb), ("wa_sb", wa), ("wb_sb", wb), ("fa_sb", fa), ("fb_sb", fb))
+        )
+
+        x_codes0 = keep.tile([P, S], U32, align_bytes=64)
+        nc.vector.tensor_copy(x_codes0[:], word_table[0][:].bitcast(U32).indirect(offs_sb[:]))
+        x_scale = keep.tile([P, S], U8, align_bytes=64)
+        nc.vector.tensor_copy(x_scale[:], scale_table[:].indirect(offs_sb[:]))
+
+        def interleave(engine_copy, a, b):
+            grouped = keep.tile([P, P * PACK], BF16, name=f"w_grouped{a}{b}", align_bytes=64)
+            engine_copy(
+                grouped[:].rearrange("p (c i t) -> p c t i", i=4, t=PACK),
+                w_raw[a][:, :, b * P : (b + 1) * P].rearrange("p t (c i) -> p c t i", i=4),
+            )
+            return grouped
+
+        def scalar_copy(dst, src):
+            nc.scalar.activation(dst, src, COPY)
+
+        grouped = {}
+        grouped[0, 0] = interleave(scalar_copy, 0, 0)
+        grouped[0, 1] = interleave(scalar_copy, 0, 1)
+        grouped[1, 0] = interleave(nc.vector.tensor_copy, 1, 0)
+        grouped[1, 1] = interleave(scalar_copy, 1, 1)
+        w_codes, w_scale = {}, {}
+        for a in range(PASSES):
+            for b in range(BLOCKS):
+                codes = keep.tile([P, P], U32, name=f"w_codes{a}{b}", align_bytes=64)
+                scale = keep.tile([P, P], U8, name=f"w_scale{a}{b}", align_bytes=64)
+                nc.vector.quantize_mx(out=codes[:].bitcast(FP8X4), scales=scale[:], in_=grouped[a, b][:])
+                w_codes[a, b], w_scale[a, b] = codes, scale
+
+        acc = {
+            (b, lo): psum.tile([P, hi - lo], F32, name=f"acc{b}_{lo}") for b in range(BLOCKS) for lo, hi in PIECES
+        }
+
+        def product(a, b, lo, hi, codes):
+            nc.tensor.matmul_mx(
+                out=acc[b, lo][:],
+                lhsT=w_codes[a, b][:].bitcast(FP8X4),
+                lhsT_scale=w_scale[a, b][:],
+                rhs=codes.bitcast(FP8X4),
+                rhs_scale=x_scale[4 * a : P, lo:hi],
+                start=(a == 0),
+                stop=(a == PASSES - 1),
+            )
+
+        for b in range(BLOCKS):
+            for lo, hi in PIECES:
+                product(0, b, lo, hi, x_codes0[:, lo:hi])
+
+        ends = [keep.tile([P, S], F32, name=f"ends{b}") for b in range(BLOCKS)]
+        wings = [keep.tile([P, S], F32, name=f"wings{b}") for b in range(BLOCKS)]
+        fine = [keep.tile([P, W], F32, name=f"fine{b}") for b in range(BLOCKS)]
+        for lo, hi in PIECES:
+            piece = keep.tile([P, hi - lo], U32, name=f"x_codes1_{lo}", align_bytes=64)
+            nc.vector.tensor_copy(piece[:], word_table[1][:].bitcast(U32).indirect(entries(offs_sb, lo, hi)))
+            for b in range(BLOCKS):
+                product(1, b, lo, hi, piece[:])
+                nc.scalar.activation(ends[b][:, lo:hi], acc[b, lo][:], COPY, scale=0.375)
+        for window, factor in ((wings, 0.125), (fine, 1.0)):
+            for b in range(BLOCKS):
+                for lo, hi in PIECES:
+                    nc.scalar.activation(window[b][:, lo:hi], acc[b, lo][:], COPY, scale=factor)
+
+        part = {}
+        for step, (window, list_tile) in enumerate(((ends, ea_sb), (ends, eb_sb), (wings, wa_sb), (wings, wb_sb))):
+            for b in range(BLOCKS):
+                picked = window[b][:].indirect(list_tile[:])
+                if step == 3:
+                    target = fine[b][:, S:W]
+                else:
+                    target = keep.tile([P, V], F32, name=f"part{b}_{step}")[:]
+                if step == 0:
+                    nc.vector.tensor_copy(target, picked)
+                else:
+                    nc.vector.tensor_tensor(target, picked, part[b], ALU.add)
+                part[b] = target
+
+        for b in range(BLOCKS):
+            halves = range(0, U, HALF)
+            first = {lo: keep.tile([P, HALF], F32, name=f"first{b}_{lo}") for lo in halves}
+            diff = {lo: keep.tile([P, HALF], F32, name=f"diff{b}_{lo}") for lo in halves}
+            bent = {lo: keep.tile([P, HALF], F32, name=f"bent{b}_{lo}") for lo in halves}
+            result = {lo: keep.tile([P, HALF], F32, name=f"result{b}_{lo}") for lo in halves}
+            for lo in halves:
+                nc.vector.tensor_copy(first[lo][:], fine[b][:].indirect(entries(fa_sb, lo, lo + HALF)))
+            for lo in halves:
+                nc.vector.tensor_tensor(
+                    diff[lo][:], fine[b][:].indirect(entries(fb_sb, lo, lo + HALF)), first[lo][:], ALU.subtract
+                )
+            for lo in halves:
+                nc.vector.scalar_tensor_tensor(bent[lo][:], diff[lo][:], 3.0, diff[lo][:], ALU.mult, ALU.max)
+            for lo in halves:
+                nc.vector.scalar_tensor_tensor(result[lo][:], bent[lo][:], 0.25, first[lo][:], ALU.mult, ALU.add)
+                nc.sync.dma_start(out[b * P : (b + 1) * P, lo : lo + HALF], result[lo][:])

@@ -1,6 +1,7 @@
 from contextlib import ExitStack
 
 import concourse.mybir as mybir
+from concourse.masks import make_identity
 
 K, T, S, N, V, W, U = 1024, 1024, 512, 256, 256, 768, 512
 FLOPS = 2 * K * S * N
@@ -14,6 +15,7 @@ U8 = mybir.dt.uint8
 FP8X4 = mybir.dt.float8_e4m3fn_x4
 ALU = mybir.AluOpType
 COPY = mybir.ActivationFunctionType.Copy
+ABS = mybir.ActivationFunctionType.Abs
 
 P = 128
 PACK = 4
@@ -21,6 +23,7 @@ PASSES = K // (P * PACK)
 BLOCKS = N // P
 PIECES = ((0, 256), (256, 384), (384, 512))
 HALF = U // 2
+FINE_SCALE = (0.5, 1.0)
 
 
 def entries(list_tile, lo, hi):
@@ -40,12 +43,8 @@ def tile_picked_yloopsd_fine_p_kernel(tc, x_words, x_scales, w1, offs, ea, eb, w
 
         scale_table = keep.tile([P, T], U8, align_bytes=64)
         nc.vector.memset(scale_table[:].bitcast(I32), 0)
-        offs_sb = load_list("offs_sb", offs)
-        for q in range(4):
-            nc.sync.dma_start(
-                scale_table[32 * q : 32 * q + 4 * PASSES, :].bitcast(I32),
-                x_scales[:, 4 * q : 4 * q + 4, :].bitcast(I32),
-            )
+        identity = keep.tile([P, P], F32)
+        make_identity(nc, identity[:])
 
         word_table = [keep.tile([P, T], I32, name=f"word_table{a}", align_bytes=64) for a in range(PASSES)]
         w_raw = [keep.tile([P, PACK, N], F32, name=f"w_raw{a}", align_bytes=64) for a in range(PASSES)]
@@ -54,6 +53,12 @@ def tile_picked_yloopsd_fine_p_kernel(tc, x_words, x_scales, w1, offs, ea, eb, w
             nc.sync.dma_start(word_table[a][:], x_words[a].rearrange("p n t -> p (n t)").bitcast(I32))
 
         load_words(0)
+        offs_sb = load_list("offs_sb", offs)
+        for q in range(4):
+            nc.sync.dma_start(
+                scale_table[32 * q : 32 * q + 4 * PASSES, :].bitcast(I32),
+                x_scales[:, 4 * q : 4 * q + 4, :].bitcast(I32),
+            )
         for a in range(PASSES):
             nc.sync.dma_start(w_raw[a][:], w1[a * 512 : (a + 1) * 512, :].rearrange("(p j) m -> p j m", j=PACK))
         load_words(1)
@@ -67,8 +72,8 @@ def tile_picked_yloopsd_fine_p_kernel(tc, x_words, x_scales, w1, offs, ea, eb, w
         x_scale = keep.tile([P, S], U8, align_bytes=64)
         nc.vector.tensor_copy(x_scale[:], scale_table[:].indirect(offs_sb[:]))
 
-        def interleave(engine_copy, a, b):
-            grouped = keep.tile([P, P * PACK], BF16, name=f"w_grouped{a}{b}", align_bytes=64)
+        def interleave(engine_copy, a, b, tag):
+            grouped = keep.tile([P, P * PACK], BF16, name=f"w_grouped{a}{b}", tag=tag, align_bytes=64)
             engine_copy(
                 grouped[:].rearrange("p (c i t) -> p c t i", i=4, t=PACK),
                 w_raw[a][:, :, b * P : (b + 1) * P].rearrange("p t (c i) -> p c t i", i=4),
@@ -78,17 +83,13 @@ def tile_picked_yloopsd_fine_p_kernel(tc, x_words, x_scales, w1, offs, ea, eb, w
         def scalar_copy(dst, src):
             nc.scalar.activation(dst, src, COPY)
 
-        grouped = {}
-        grouped[0, 0] = interleave(scalar_copy, 0, 0)
-        grouped[0, 1] = interleave(scalar_copy, 0, 1)
-        grouped[1, 0] = interleave(nc.vector.tensor_copy, 1, 0)
-        grouped[1, 1] = interleave(scalar_copy, 1, 1)
         w_codes, w_scale = {}, {}
-        for a in range(PASSES):
+        for a, tags in enumerate((("staged_a", "staged_b"), ("staged_b", "staged_c"))):
+            grouped = [interleave(copy, a, b, tags[b]) for b, copy in enumerate((nc.vector.tensor_copy, scalar_copy))]
             for b in range(BLOCKS):
                 codes = keep.tile([P, P], U32, name=f"w_codes{a}{b}", align_bytes=64)
                 scale = keep.tile([P, P], U8, name=f"w_scale{a}{b}", align_bytes=64)
-                nc.vector.quantize_mx(out=codes[:].bitcast(FP8X4), scales=scale[:], in_=grouped[a, b][:])
+                nc.vector.quantize_mx(out=codes[:].bitcast(FP8X4), scales=scale[:], in_=grouped[b][:])
                 w_codes[a, b], w_scale[a, b] = codes, scale
 
         acc = {
@@ -113,16 +114,16 @@ def tile_picked_yloopsd_fine_p_kernel(tc, x_words, x_scales, w1, offs, ea, eb, w
         ends = [keep.tile([P, S], F32, name=f"ends{b}") for b in range(BLOCKS)]
         wings = [keep.tile([P, S], F32, name=f"wings{b}") for b in range(BLOCKS)]
         fine = [keep.tile([P, W], F32, name=f"fine{b}") for b in range(BLOCKS)]
-        for lo, hi in PIECES:
-            piece = keep.tile([P, hi - lo], U32, name=f"x_codes1_{lo}", align_bytes=64)
+        for (lo, hi), tag in zip(PIECES, ("staged_c", "x_codes1_mid", "x_codes1_end")):
+            piece = keep.tile([P, hi - lo], U32, name=f"x_codes1_{lo}", tag=tag, align_bytes=64)
             nc.vector.tensor_copy(piece[:], word_table[1][:].bitcast(U32).indirect(entries(offs_sb, lo, hi)))
             for b in range(BLOCKS):
                 product(1, b, lo, hi, piece[:])
-                nc.scalar.activation(ends[b][:, lo:hi], acc[b, lo][:], COPY, scale=0.375)
+                nc.scalar.activation(ends[b][:, lo:hi], acc[b, lo][:], COPY, scale=0.375 * FINE_SCALE[b])
         for window, factor in ((wings, 0.125), (fine, 1.0)):
             for b in range(BLOCKS):
                 for lo, hi in PIECES:
-                    nc.scalar.activation(window[b][:, lo:hi], acc[b, lo][:], COPY, scale=factor)
+                    nc.scalar.activation(window[b][:, lo:hi], acc[b, lo][:], COPY, scale=factor * FINE_SCALE[b])
 
         part = {}
         for step, (window, list_tile) in enumerate(((ends, ea_sb), (ends, eb_sb), (wings, wa_sb), (wings, wb_sb))):
@@ -138,20 +139,44 @@ def tile_picked_yloopsd_fine_p_kernel(tc, x_words, x_scales, w1, offs, ea, eb, w
                     nc.vector.tensor_tensor(target, picked, part[b], ALU.add)
                 part[b] = target
 
+        halves = range(0, U, HALF)
+        first, diff = {}, {}
         for b in range(BLOCKS):
-            halves = range(0, U, HALF)
-            first = {lo: keep.tile([P, HALF], F32, name=f"first{b}_{lo}") for lo in halves}
-            diff = {lo: keep.tile([P, HALF], F32, name=f"diff{b}_{lo}") for lo in halves}
-            bent = {lo: keep.tile([P, HALF], F32, name=f"bent{b}_{lo}") for lo in halves}
-            result = {lo: keep.tile([P, HALF], F32, name=f"result{b}_{lo}") for lo in halves}
             for lo in halves:
-                nc.vector.tensor_copy(first[lo][:], fine[b][:].indirect(entries(fa_sb, lo, lo + HALF)))
+                first[b, lo] = keep.tile([P, HALF], F32, name=f"first{b}_{lo}")
+                nc.vector.tensor_copy(first[b, lo][:], fine[b][:].indirect(entries(fa_sb, lo, lo + HALF)))
             for lo in halves:
+                diff[b, lo] = keep.tile([P, HALF], F32, name=f"diff{b}_{lo}")
                 nc.vector.tensor_tensor(
-                    diff[lo][:], fine[b][:].indirect(entries(fb_sb, lo, lo + HALF)), first[lo][:], ALU.subtract
+                    diff[b, lo][:], fine[b][:].indirect(entries(fb_sb, lo, lo + HALF)), first[b, lo][:], ALU.subtract
                 )
-            for lo in halves:
-                nc.vector.scalar_tensor_tensor(bent[lo][:], diff[lo][:], 3.0, diff[lo][:], ALU.mult, ALU.max)
-            for lo in halves:
-                nc.vector.scalar_tensor_tensor(result[lo][:], bent[lo][:], 0.25, first[lo][:], ALU.mult, ALU.add)
-                nc.sync.dma_start(out[b * P : (b + 1) * P, lo : lo + HALF], result[lo][:])
+
+        sum_banks = {0: ("sum_a", "sum_b", "acc0_384"), HALF: ("acc0_0", "acc0_256", "acc1_0")}
+        for lo in halves:
+            extent = keep.tile([P, HALF], F32, name=f"extent{lo}")
+            nc.scalar.activation(extent[:], diff[0, lo][:], ABS, scale=0.5)
+            turned = keep.tile([P, HALF], F32, name=f"turned{lo}")
+            for t in range(HALF // P):
+                cols = slice(t * P, (t + 1) * P)
+                total = psum.tile([P, P], F32, name=f"total{lo}_{t}", tag=sum_banks[lo][t])
+                terms = (first[0, lo], first[0, lo], diff[0, lo], extent)
+                for n, term in enumerate(terms):
+                    nc.tensor.matmul(
+                        total[:], term[:, cols], identity[:], start=(n == 0), stop=(n == len(terms) - 1), is_transpose=True
+                    )
+                nc.scalar.copy(turned[:, cols], total[:])
+            back = psum.tile([P, HALF], F32, name=f"back{lo}", tag=sum_banks[lo][2])
+            for t in range(HALF // P):
+                cols = slice(t * P, (t + 1) * P)
+                nc.tensor.transpose(back[:, cols], turned[:, cols], identity[:])
+            result = keep.tile([P, HALF], F32, name=f"result0_{lo}")
+            nc.scalar.copy(result[:], back[:])
+            nc.sync.dma_start(out[0:P, lo : lo + HALF], result[:])
+
+        bent = {lo: keep.tile([P, HALF], F32, name=f"bent{lo}") for lo in halves}
+        for lo in halves:
+            nc.vector.scalar_tensor_tensor(bent[lo][:], diff[1, lo][:], 3.0, diff[1, lo][:], ALU.mult, ALU.max)
+        for lo in halves:
+            result = keep.tile([P, HALF], F32, name=f"result1_{lo}")
+            nc.vector.scalar_tensor_tensor(result[:], bent[lo][:], 0.25, first[1, lo][:], ALU.mult, ALU.add)
+            nc.sync.dma_start(out[P : 2 * P, lo : lo + HALF], result[:])

@@ -141,9 +141,10 @@ def tile_picked_yloopsd_fine_p_kernel(tc, x_words, x_scales, w1, offs, ea, eb, w
 
         halves = range(0, U, HALF)
         first, diff = {}, {}
-        for b in range(BLOCKS):
+
+        def fetch(b):
             for lo in halves:
-                first[b, lo] = keep.tile([P, HALF], F32, name=f"first{b}_{lo}")
+                first[b, lo] = keep.tile([P, HALF], F32, name=f"first{b}_{lo}", tag=f"first_{lo}")
                 nc.vector.tensor_copy(first[b, lo][:], fine[b][:].indirect(entries(fa_sb, lo, lo + HALF)))
             for lo in halves:
                 diff[b, lo] = keep.tile([P, HALF], F32, name=f"diff{b}_{lo}")
@@ -151,28 +152,31 @@ def tile_picked_yloopsd_fine_p_kernel(tc, x_words, x_scales, w1, offs, ea, eb, w
                     diff[b, lo][:], fine[b][:].indirect(entries(fb_sb, lo, lo + HALF)), first[b, lo][:], ALU.subtract
                 )
 
-        sum_banks = {0: ("sum_a", "sum_b", "acc0_384"), HALF: ("acc0_0", "acc0_256", "acc1_0")}
+        fetch(0)
+        total_tags = ("sum_a", "sum_b", "acc0_0", "acc0_256")
+        squares = [slice(c, c + P) for c in range(0, HALF, P)]
         for lo in halves:
+            doubled = keep.tile([P, HALF], F32, name=f"doubled{lo}")
+            nc.scalar.activation(doubled[:], first[0, lo][:], COPY, scale=2.0)
             extent = keep.tile([P, HALF], F32, name=f"extent{lo}")
             nc.scalar.activation(extent[:], diff[0, lo][:], ABS, scale=0.5)
+            terms = (doubled, diff[0, lo], extent)
             turned = keep.tile([P, HALF], F32, name=f"turned{lo}")
-            for t in range(HALF // P):
-                cols = slice(t * P, (t + 1) * P)
-                total = psum.tile([P, P], F32, name=f"total{lo}_{t}", tag=sum_banks[lo][t])
-                terms = (first[0, lo], first[0, lo], diff[0, lo], extent)
+            for cols in squares:
+                total = psum.tile([P, P], F32, name=f"total{lo + cols.start}", tag=total_tags[(lo + cols.start) // P])
                 for n, term in enumerate(terms):
                     nc.tensor.matmul(
                         total[:], term[:, cols], identity[:], start=(n == 0), stop=(n == len(terms) - 1), is_transpose=True
                     )
                 nc.scalar.copy(turned[:, cols], total[:])
-            back = psum.tile([P, HALF], F32, name=f"back{lo}", tag=sum_banks[lo][2])
-            for t in range(HALF // P):
-                cols = slice(t * P, (t + 1) * P)
+            back = psum.tile([P, HALF], F32, name=f"back{lo}", tag=f"acc1_{lo}")
+            for cols in squares:
                 nc.tensor.transpose(back[:, cols], turned[:, cols], identity[:])
             result = keep.tile([P, HALF], F32, name=f"result0_{lo}")
             nc.scalar.copy(result[:], back[:])
-            nc.sync.dma_start(out[0:P, lo : lo + HALF], result[:])
+            nc.scalar.dma_start(out[0:P, lo : lo + HALF], result[:])
 
+        fetch(1)
         bent = {lo: keep.tile([P, HALF], F32, name=f"bent{lo}") for lo in halves}
         for lo in halves:
             nc.vector.scalar_tensor_tensor(bent[lo][:], diff[1, lo][:], 3.0, diff[1, lo][:], ALU.mult, ALU.max)

@@ -21,7 +21,8 @@ P = 128
 PACK = 4
 PASSES = K // (P * PACK)
 BLOCKS = N // P
-PIECES = ((0, 256), (256, 384), (384, 512))
+LAST = 384
+PIECES = (((0, 256), (256, LAST), (LAST, 512)),) * 2
 HALF = U // 2
 FINE_SCALE = (0.5, 1.0)
 
@@ -47,82 +48,94 @@ def tile_picked_yloopsd_fine_p_kernel(tc, x_words, x_scales, w1, offs, ea, eb, w
         make_identity(nc, identity[:])
 
         word_table = [keep.tile([P, T], I32, name=f"word_table{a}", align_bytes=64) for a in range(PASSES)]
-        w_raw = [keep.tile([P, PACK, N], F32, name=f"w_raw{a}", align_bytes=64) for a in range(PASSES)]
+        w_raw0 = keep.tile([P, PACK, N], F32, align_bytes=64)
+        w_raw1 = [keep.tile([P, PACK, P], F32, name=f"w_raw1{b}", align_bytes=64) for b in range(BLOCKS)]
+        w_rows = w1.rearrange("(a p j) m -> a p j m", a=PASSES, j=PACK)
 
         def load_words(a):
             nc.sync.dma_start(word_table[a][:], x_words[a].rearrange("p n t -> p (n t)").bitcast(I32))
 
         load_words(0)
         offs_sb = load_list("offs_sb", offs)
+        nc.sync.dma_start(w_raw0[:], w_rows[0])
         for q in range(4):
             nc.sync.dma_start(
                 scale_table[32 * q : 32 * q + 4 * PASSES, :].bitcast(I32),
                 x_scales[:, 4 * q : 4 * q + 4, :].bitcast(I32),
             )
-        for a in range(PASSES):
-            nc.sync.dma_start(w_raw[a][:], w1[a * 512 : (a + 1) * 512, :].rearrange("(p j) m -> p j m", j=PACK))
+        nc.sync.dma_start(w_raw1[0][:], w_rows[1][:, :, 0:P])
         load_words(1)
+        nc.sync.dma_start(w_raw1[1][:], w_rows[1][:, :, P:N])
         ea_sb, eb_sb, wa_sb, wb_sb, fa_sb, fb_sb = (
             load_list(name, src)
             for name, src in (("ea_sb", ea), ("eb_sb", eb), ("wa_sb", wa), ("wb_sb", wb), ("fa_sb", fa), ("fb_sb", fb))
         )
 
-        x_codes0 = keep.tile([P, S], U32, align_bytes=64)
-        nc.vector.tensor_copy(x_codes0[:], word_table[0][:].bitcast(U32).indirect(offs_sb[:]))
+        def pick_words(a, lo, hi, tag):
+            x_codes = keep.tile([P, hi - lo], U32, name=f"x_codes{a}_{lo}", tag=tag, align_bytes=64)
+            nc.vector.tensor_copy(x_codes[:], word_table[a][:].bitcast(U32).indirect(entries(offs_sb, lo, hi)))
+            return x_codes
+
+        x_codes0 = pick_words(0, 0, S, "x_codes0")
         x_scale = keep.tile([P, S], U8, align_bytes=64)
         nc.vector.tensor_copy(x_scale[:], scale_table[:].indirect(offs_sb[:]))
 
-        def interleave(engine_copy, a, b, tag):
-            grouped = keep.tile([P, P * PACK], BF16, name=f"w_grouped{a}{b}", tag=tag, align_bytes=64)
-            engine_copy(
+        def interleave(raw, name):
+            grouped = keep.tile([P, raw.shape[2] * PACK], BF16, name=name, align_bytes=64)
+            nc.scalar.activation(
                 grouped[:].rearrange("p (c i t) -> p c t i", i=4, t=PACK),
-                w_raw[a][:, :, b * P : (b + 1) * P].rearrange("p t (c i) -> p c t i", i=4),
+                raw[:].rearrange("p t (c i) -> p c t i", i=4),
+                COPY,
             )
             return grouped
 
-        def scalar_copy(dst, src):
-            nc.scalar.activation(dst, src, COPY)
-
-        w_codes, w_scale = {}, {}
-        for a, tags in enumerate((("staged_a", "staged_b"), ("staged_b", "staged_c"))):
-            grouped = [interleave(copy, a, b, tags[b]) for b, copy in enumerate((nc.vector.tensor_copy, scalar_copy))]
-            for b in range(BLOCKS):
-                codes = keep.tile([P, P], U32, name=f"w_codes{a}{b}", align_bytes=64)
-                scale = keep.tile([P, P], U8, name=f"w_scale{a}{b}", align_bytes=64)
-                nc.vector.quantize_mx(out=codes[:].bitcast(FP8X4), scales=scale[:], in_=grouped[b][:])
-                w_codes[a, b], w_scale[a, b] = codes, scale
+        def quantize(grouped, name, tag):
+            width = grouped.shape[1] // PACK
+            codes = keep.tile([P, width], U32, name=f"w_codes{name}", tag=tag, align_bytes=64)
+            scale = keep.tile([P, width], U8, name=f"w_scale{name}", align_bytes=64)
+            nc.vector.quantize_mx(out=codes[:].bitcast(FP8X4), scales=scale[:], in_=grouped[:])
+            return codes, scale
 
         acc = {
-            (b, lo): psum.tile([P, hi - lo], F32, name=f"acc{b}_{lo}") for b in range(BLOCKS) for lo, hi in PIECES
+            (b, lo): psum.tile([P, hi - lo], F32, name=f"acc{b}_{lo}") for b in range(BLOCKS) for lo, hi in PIECES[b]
         }
 
-        def product(a, b, lo, hi, codes):
+        def product(a, b, lo, hi, w_codes, w_scale, x_codes):
             nc.tensor.matmul_mx(
                 out=acc[b, lo][:],
-                lhsT=w_codes[a, b][:].bitcast(FP8X4),
-                lhsT_scale=w_scale[a, b][:],
-                rhs=codes.bitcast(FP8X4),
+                lhsT=w_codes.bitcast(FP8X4),
+                lhsT_scale=w_scale,
+                rhs=x_codes.bitcast(FP8X4),
                 rhs_scale=x_scale[4 * a : P, lo:hi],
                 start=(a == 0),
                 stop=(a == PASSES - 1),
             )
 
+        grouped0 = interleave(w_raw0, "grouped0")
+        grouped1 = [interleave(w_raw1[b], f"grouped1{b}") for b in range(BLOCKS)]
+
+        w_codes, w_scale = quantize(grouped0, "0", "w_codes0")
         for b in range(BLOCKS):
-            for lo, hi in PIECES:
-                product(0, b, lo, hi, x_codes0[:, lo:hi])
+            cols = slice(b * P, (b + 1) * P)
+            for lo, hi in PIECES[b]:
+                product(0, b, lo, hi, w_codes[:, cols], w_scale[:, cols], x_codes0[:, lo:hi])
+
+        w_codes, w_scale = quantize(grouped1[0], "10", "w_codes10")
+        head = pick_words(1, 0, LAST, "w_raw10")
+        last = pick_words(1, LAST, S, "grouped10")
+        for b in range(BLOCKS):
+            if b == 1:
+                w_codes, w_scale = quantize(grouped1[1], "11", "word_table1")
+            for lo, hi in PIECES[b]:
+                x_codes = head[:, lo:hi] if lo < LAST else last[:]
+                product(1, b, lo, hi, w_codes[:], w_scale[:], x_codes)
 
         ends = [keep.tile([P, S], F32, name=f"ends{b}") for b in range(BLOCKS)]
         wings = [keep.tile([P, S], F32, name=f"wings{b}") for b in range(BLOCKS)]
         fine = [keep.tile([P, W], F32, name=f"fine{b}") for b in range(BLOCKS)]
-        for (lo, hi), tag in zip(PIECES, ("staged_c", "x_codes1_mid", "x_codes1_end")):
-            piece = keep.tile([P, hi - lo], U32, name=f"x_codes1_{lo}", tag=tag, align_bytes=64)
-            nc.vector.tensor_copy(piece[:], word_table[1][:].bitcast(U32).indirect(entries(offs_sb, lo, hi)))
+        for window, factor in ((ends, 0.375), (wings, 0.125), (fine, 1.0)):
             for b in range(BLOCKS):
-                product(1, b, lo, hi, piece[:])
-                nc.scalar.activation(ends[b][:, lo:hi], acc[b, lo][:], COPY, scale=0.375 * FINE_SCALE[b])
-        for window, factor in ((wings, 0.125), (fine, 1.0)):
-            for b in range(BLOCKS):
-                for lo, hi in PIECES:
+                for lo, hi in PIECES[b]:
                     nc.scalar.activation(window[b][:, lo:hi], acc[b, lo][:], COPY, scale=factor * FINE_SCALE[b])
 
         part = {}

from contextlib import ExitStack

import concourse.mybir as mybir
from concourse.masks import make_identity

K, T, S, N, V, W, U = 1024, 1024, 512, 256, 256, 768, 512
FLOPS = 2 * K * S * N

F32 = mybir.dt.float32
BF16 = mybir.dt.bfloat16
I32 = mybir.dt.int32
U32 = mybir.dt.uint32
U16 = mybir.dt.uint16
U8 = mybir.dt.uint8
FP8X4 = mybir.dt.float8_e4m3fn_x4
ALU = mybir.AluOpType
COPY = mybir.ActivationFunctionType.Copy
ABS = mybir.ActivationFunctionType.Abs

P = 128
PACK = 4
PASSES = K // (P * PACK)
BLOCKS = N // P
LAST = 384
PIECES = (((0, 256), (256, LAST), (LAST, 512)),) * 2
HALF = U // 2
FINE_SCALE = (0.5, 1.0)


def entries(list_tile, lo, hi):
    return list_tile[:, lo // 16 : hi // 16]


def tile_picked_yloopsd_fine_p_kernel(tc, x_words, x_scales, w1, offs, ea, eb, wa, wb, fa, fb, out):
    nc = tc.nc
    with ExitStack() as ctx:
        keep = ctx.enter_context(tc.tile_pool(name="keep", bufs=1))
        psum = ctx.enter_context(tc.psum_pool(name="psum", bufs=1))

        def load_list(name, src):
            tile = keep.tile([P, src.shape[1]], U16, name=name)
            nc.sync.dma_start(tile[:], src)
            return tile

        scale_table = keep.tile([P, T], U8, align_bytes=64)
        nc.vector.memset(scale_table[:].bitcast(I32), 0)
        identity = keep.tile([P, P], F32)
        make_identity(nc, identity[:])

        word_table = [keep.tile([P, T], I32, name=f"word_table{a}", align_bytes=64) for a in range(PASSES)]
        w_raw0 = keep.tile([P, PACK, N], F32, align_bytes=64)
        w_raw1 = [keep.tile([P, PACK, P], F32, name=f"w_raw1{b}", align_bytes=64) for b in range(BLOCKS)]
        w_rows = w1.rearrange("(a p j) m -> a p j m", a=PASSES, j=PACK)

        def load_words(a):
            nc.sync.dma_start(word_table[a][:], x_words[a].rearrange("p n t -> p (n t)").bitcast(I32))

        load_words(0)
        offs_sb = load_list("offs_sb", offs)
        nc.sync.dma_start(w_raw0[:], w_rows[0])
        for q in range(4):
            nc.sync.dma_start(
                scale_table[32 * q : 32 * q + 4 * PASSES, :].bitcast(I32),
                x_scales[:, 4 * q : 4 * q + 4, :].bitcast(I32),
            )
        nc.sync.dma_start(w_raw1[0][:], w_rows[1][:, :, 0:P])
        load_words(1)
        nc.sync.dma_start(w_raw1[1][:], w_rows[1][:, :, P:N])
        ea_sb, eb_sb, wa_sb, wb_sb, fa_sb, fb_sb = (
            load_list(name, src)
            for name, src in (("ea_sb", ea), ("eb_sb", eb), ("wa_sb", wa), ("wb_sb", wb), ("fa_sb", fa), ("fb_sb", fb))
        )

        def pick_words(a, lo, hi, tag):
            x_codes = keep.tile([P, hi - lo], U32, name=f"x_codes{a}_{lo}", tag=tag, align_bytes=64)
            nc.vector.tensor_copy(x_codes[:], word_table[a][:].bitcast(U32).indirect(entries(offs_sb, lo, hi)))
            return x_codes

        x_codes0 = pick_words(0, 0, S, "x_codes0")
        x_scale = keep.tile([P, S], U8, align_bytes=64)
        nc.vector.tensor_copy(x_scale[:], scale_table[:].indirect(offs_sb[:]))

        def interleave(raw, name):
            grouped = keep.tile([P, raw.shape[2] * PACK], BF16, name=name, align_bytes=64)
            nc.scalar.activation(
                grouped[:].rearrange("p (c i t) -> p c t i", i=4, t=PACK),
                raw[:].rearrange("p t (c i) -> p c t i", i=4),
                COPY,
            )
            return grouped

        def quantize(grouped, name, tag):
            width = grouped.shape[1] // PACK
            codes = keep.tile([P, width], U32, name=f"w_codes{name}", tag=tag, align_bytes=64)
            scale = keep.tile([P, width], U8, name=f"w_scale{name}", align_bytes=64)
            nc.vector.quantize_mx(out=codes[:].bitcast(FP8X4), scales=scale[:], in_=grouped[:])
            return codes, scale

        acc = {
            (b, lo): psum.tile([P, hi - lo], F32, name=f"acc{b}_{lo}") for b in range(BLOCKS) for lo, hi in PIECES[b]
        }

        def product(a, b, lo, hi, w_codes, w_scale, x_codes):
            nc.tensor.matmul_mx(
                out=acc[b, lo][:],
                lhsT=w_codes.bitcast(FP8X4),
                lhsT_scale=w_scale,
                rhs=x_codes.bitcast(FP8X4),
                rhs_scale=x_scale[4 * a : P, lo:hi],
                start=(a == 0),
                stop=(a == PASSES - 1),
            )

        grouped0 = interleave(w_raw0, "grouped0")
        grouped1 = [interleave(w_raw1[b], f"grouped1{b}") for b in range(BLOCKS)]

        w_codes, w_scale = quantize(grouped0, "0", "w_codes0")
        for b in range(BLOCKS):
            cols = slice(b * P, (b + 1) * P)
            for lo, hi in PIECES[b]:
                product(0, b, lo, hi, w_codes[:, cols], w_scale[:, cols], x_codes0[:, lo:hi])

        w_codes, w_scale = quantize(grouped1[0], "10", "w_codes10")
        head = pick_words(1, 0, LAST, "w_raw10")
        last = pick_words(1, LAST, S, "grouped10")
        for b in range(BLOCKS):
            if b == 1:
                w_codes, w_scale = quantize(grouped1[1], "11", "word_table1")
            for lo, hi in PIECES[b]:
                x_codes = head[:, lo:hi] if lo < LAST else last[:]
                product(1, b, lo, hi, w_codes[:], w_scale[:], x_codes)

        ends = [keep.tile([P, S], F32, name=f"ends{b}") for b in range(BLOCKS)]
        wings = [keep.tile([P, S], F32, name=f"wings{b}") for b in range(BLOCKS)]
        fine = [keep.tile([P, W], F32, name=f"fine{b}") for b in range(BLOCKS)]
        for window, factor in ((ends, 0.375), (wings, 0.125), (fine, 1.0)):
            for b in range(BLOCKS):
                for lo, hi in PIECES[b]:
                    nc.scalar.activation(window[b][:, lo:hi], acc[b, lo][:], COPY, scale=factor * FINE_SCALE[b])

        part = {}
        for step, (window, list_tile) in enumerate(((ends, ea_sb), (ends, eb_sb), (wings, wa_sb), (wings, wb_sb))):
            for b in range(BLOCKS):
                picked = window[b][:].indirect(list_tile[:])
                if step == 3:
                    target = fine[b][:, S:W]
                else:
                    target = keep.tile([P, V], F32, name=f"part{b}_{step}")[:]
                if step == 0:
                    nc.vector.tensor_copy(target, picked)
                else:
                    nc.vector.tensor_tensor(target, picked, part[b], ALU.add)
                part[b] = target

        halves = range(0, U, HALF)
        first, diff = {}, {}

        def fetch(b):
            for lo in halves:
                first[b, lo] = keep.tile([P, HALF], F32, name=f"first{b}_{lo}", tag=f"first_{lo}")
                nc.vector.tensor_copy(first[b, lo][:], fine[b][:].indirect(entries(fa_sb, lo, lo + HALF)))
            for lo in halves:
                diff[b, lo] = keep.tile([P, HALF], F32, name=f"diff{b}_{lo}")
                nc.vector.tensor_tensor(
                    diff[b, lo][:], fine[b][:].indirect(entries(fb_sb, lo, lo + HALF)), first[b, lo][:], ALU.subtract
                )

        fetch(0)
        total_tags = ("sum_a", "sum_b", "acc0_0", "acc0_256")
        squares = [slice(c, c + P) for c in range(0, HALF, P)]
        for lo in halves:
            doubled = keep.tile([P, HALF], F32, name=f"doubled{lo}")
            nc.scalar.activation(doubled[:], first[0, lo][:], COPY, scale=2.0)
            extent = keep.tile([P, HALF], F32, name=f"extent{lo}")
            nc.scalar.activation(extent[:], diff[0, lo][:], ABS, scale=0.5)
            terms = (doubled, diff[0, lo], extent)
            turned = keep.tile([P, HALF], F32, name=f"turned{lo}")
            for cols in squares:
                total = psum.tile([P, P], F32, name=f"total{lo + cols.start}", tag=total_tags[(lo + cols.start) // P])
                for n, term in enumerate(terms):
                    nc.tensor.matmul(
                        total[:], term[:, cols], identity[:], start=(n == 0), stop=(n == len(terms) - 1), is_transpose=True
                    )
                nc.scalar.copy(turned[:, cols], total[:])
            back = psum.tile([P, HALF], F32, name=f"back{lo}", tag=f"acc1_{lo}")
            for cols in squares:
                nc.tensor.transpose(back[:, cols], turned[:, cols], identity[:])
            result = keep.tile([P, HALF], F32, name=f"result0_{lo}")
            nc.scalar.copy(result[:], back[:])
            nc.scalar.dma_start(out[0:P, lo : lo + HALF], result[:])

        fetch(1)
        bent = {lo: keep.tile([P, HALF], F32, name=f"bent{lo}") for lo in halves}
        for lo in halves:
            nc.vector.scalar_tensor_tensor(bent[lo][:], diff[1, lo][:], 3.0, diff[1, lo][:], ALU.mult, ALU.max)
        for lo in halves:
            result = keep.tile([P, HALF], F32, name=f"result1_{lo}")
            nc.vector.scalar_tensor_tensor(result[:], bent[lo][:], 0.25, first[1, lo][:], ALU.mult, ALU.add)
            nc.sync.dma_start(out[P : 2 * P, lo : lo + HALF], result[:])
